import numpy as np, ml_dtypes
CORES = [2,34,66,98,130,162,194,226,258,290,322,354,386,418,450,482]
N = 16
GR, GC = 4, 4
L, KA, KB, F = 4, 1, 1, 512
def setup_inputs(rng):
    return {"a": rng.standard_normal((N, 128, KA * 128), dtype=np.float32).astype(ml_dtypes.bfloat16), "b": rng.standard_normal((N, 128, KB * F), dtype=np.float32).astype(ml_dtypes.bfloat16)}
def reference(a, b):
    A, B = a.astype(np.float64), b.astype(np.float64)
    y = np.zeros((N, 128, F))
    for i in range(GR):
        for j in range(GC):
            for k in range(L):
                At = A[i * GC + k // KA][:, 128 * (k % KA):128 * (k % KA) + 128]
                Bt = B[(k // KB) * GC + j][:, F * (k % KB):F * (k % KB) + F]
                y[i * GC + j] += At.T @ Bt
    return {"y": y.astype(ml_dtypes.bfloat16 if a.dtype != np.float64 else np.float64)}

@@ -1,0 +1,123 @@
+from concourse.bass import DstId, RemoteDMATransfer
+
+GR, GC, F = 4, 4, 512
+
+SCRATCH = {
+    "astage": ("dram", [128, 128], "bfloat16"),
+    "aland": ("dram", [GC, 128, 128], "bfloat16"),
+    "abuf": ("sbuf", [128, GC * 128], "bfloat16"),
+    "bbuf": ("sbuf", [128, GR * F], "bfloat16"),
+    "ysb": ("sbuf", [128, F], "bfloat16"),
+    "acc": ("psum", [128, F], "float32"),
+}
+SEMAPHORES = ["a_st", "a_arr", "a_ld", "b0", "b1", "b2", "b3", "sent", "mm", "cp", "st"]
+
+FIRST_HOP_LEAVES_RACK = True
+
+
+def _engines(mask):
+    return bin(mask).count("1")
+
+
+def _relay(topo, col, k, q):
+    for p in range(len(col)):
+        if p in (k, q):
+            continue
+        if not (topo.may_write(col[k], col[p]) and topo.may_write(col[p], col[q])):
+            continue
+        leaves = topo.rack(topo.host(col[k])) != topo.rack(topo.host(col[p]))
+        if leaves == FIRST_HOP_LEAVES_RACK:
+            return p
+    raise ValueError("no relay")
+
+
+def rank_program(g, core, T, topo):
+    rank = T.rank_of(core)
+    if rank is None:
+        return
+    i, j = rank // GC, rank % GC
+    row = [T.cores[i * GC + k] for k in range(GC)]
+    col = [T.cores[k * GC + j] for k in range(GR)]
+    sem = T.sem
+
+    def a_blk(k):
+        return T.abuf[:, k * 128:(k + 1) * 128]
+
+    def b_blk(k):
+        return T.bbuf[:, k * F:(k + 1) * F]
+
+    def b_sem(k):
+        return sem["b%d" % k]
+
+    via = {}
+    for k in range(GR):
+        for q in range(GR):
+            if q != k and not topo.may_write(col[k], col[q]):
+                via[(k, q)] = _relay(topo, col, k, q)
+    my_relays = [p for (k, q), p in via.items() if k == i]
+    direct = [q for q in range(GR) if q != i and topo.may_write(core, col[q])]
+    direct.sort(key=lambda q: 0 if q in my_relays else 1)
+    passing = [(k, q) for (k, q), p in via.items() if p == i]
+    first = [k for (k, q) in passing]
+    order = [i] + first + [k for k in range(GR) if k != i and k not in first and (k, i) not in via] \
+        + [k for k in range(GR) if (k, i) in via]
+
+    g.sync.dma_start(T.astage[:], T.a[:]).then_inc(sem.a_st, 16)
+    g.scalar.dma_start(b_blk(i), T.b[:]).then_inc(b_sem(i), 16)
+    g.sync.dma_start(a_blk(j), T.a[:]).then_inc(sem.a_ld, 16)
+
+    sent = 0
+    peers = [c for c in row if c != core]
+    amask = topo.mask(core, peers[0])
+    for c in peers:
+        amask &= topo.mask(core, c)
+    ids = []
+    for c in peers:
+        rid, pid = topo.addr(c, core)
+        ids.append(DstId(rid=rid, pnc=pid))
+    g.wait_ge(sem.a_st, 16)
+    g.remote_dma_fused([RemoteDMATransfer(dst_ids=ids, dma_engine_mask=amask, remote_sem=sem.a_arr,
+                                          srcs=[T.astage[:]], dsts=[T.aland[j] for _ in peers], alu_op=0)],
+                       local_sem=sem.sent)
+    sent += _engines(amask)
+
+    def send_b(k, q):
+        rid, pid = topo.addr(col[q], core)
+        m = topo.mask(core, col[q])
+        g.remote_dma(b_blk(k), b_blk(k), b_sem(k), sem.sent, pid, rid, m)
+        return _engines(m)
+
+    g.wait_ge(b_sem(i), 16)
+    for q in direct:
+        sent += send_b(i, q)
+    for (k, q) in passing:
+        g.wait_ge(b_sem(k), _engines(topo.mask(col[k], core)))
+        sent += send_b(k, q)
+
+    a_in = sum(_engines(topo.mask(c, core)) for c in peers)
+    g.sync.wait_ge(sem.a_arr, a_in)
+    g.scalar.wait_ge(sem.a_arr, a_in)
+    queues = [g.scalar, g.sync]
+    n = 0
+    for k in range(GC):
+        if k != j:
+            queues[n % 2].dma_start(a_blk(k), T.aland[k]).then_inc(sem.a_ld, 16)
+            n += 1
+
+    g.tensor.wait_ge(sem.a_ld, 16 * GC)
+    for n, k in enumerate(order):
+        if k == i:
+            need = 16
+        elif (k, i) in via:
+            need = _engines(topo.mask(col[via[(k, i)]], core))
+        else:
+            need = _engines(topo.mask(col[k], core))
+        g.tensor.wait_ge(b_sem(k), need)
+        mm = g.tensor.matmul(T.acc[:], a_blk(k), b_blk(k), start=(n == 0), stop=(n == GR - 1))
+    mm.then_inc(sem.mm, 1)
+    g.vector.wait_ge(sem.mm, 1)
+    g.vector.tensor_copy(T.ysb[:], T.acc[:]).then_inc(sem.cp, 1)
+    g.sync.wait_ge(sem.cp, 1)
+    g.sync.dma_start(T.y[:], T.ysb[:]).then_inc(sem.st, 16)
+    g.sync.wait_ge(sem.st, 16)
+    g.wait_ge(sem.sent, sent)

@@ -1,6 +1,7 @@
 from concourse.bass import DstId, RemoteDMATransfer
 
 GR, GC, F = 4, 4, 512
+H = F // 2
 
 SCRATCH = {
     "astage": ("dram", [128, 128], "bfloat16"),
@@ -8,15 +9,20 @@ SCRATCH = {
     "abuf": ("sbuf", [128, GC * 128], "bfloat16"),
     "bbuf": ("sbuf", [128, GR * F], "bfloat16"),
     "ysb": ("sbuf", [128, F], "bfloat16"),
-    "acc": ("psum", [128, F], "float32"),
+    "acc0": ("psum", [128, F], "float32"),
+    "acc1": ("psum", [128, F], "float32"),
 }
-SEMAPHORES = ["a_st", "a_arr", "a_ld", "b0", "b1", "b2", "b3", "sent", "mm", "cp", "st"]
-
-FIRST_HOP_LEAVES_RACK = True
+SEMAPHORES = ["a_st", "a_arr", "a_ld", "sent", "mm0", "mm1", "cp0", "cp1", "st0", "st1"] \
+    + ["b%d_%d" % (k, h) for k in range(GR) for h in range(2)]
 
 
 def _engines(mask):
     return bin(mask).count("1")
+
+
+def _split(mask):
+    bits = [b for b in range(16) if (mask >> b) & 1]
+    return sum(1 << b for b in bits[0::2]), sum(1 << b for b in bits[1::2])
 
 
 def _relay(topo, col, k, q):
@@ -25,8 +31,7 @@ def _relay(topo, col, k, q):
             continue
         if not (topo.may_write(col[k], col[p]) and topo.may_write(col[p], col[q])):
             continue
-        leaves = topo.rack(topo.host(col[k])) != topo.rack(topo.host(col[p]))
-        if leaves == FIRST_HOP_LEAVES_RACK:
+        if topo.rack(topo.host(col[k])) != topo.rack(topo.host(col[p])):
             return p
     raise ValueError("no relay")
 
@@ -43,27 +48,24 @@ def rank_program(g, core, T, topo):
     def a_blk(k):
         return T.abuf[:, k * 128:(k + 1) * 128]
 
-    def b_blk(k):
-        return T.bbuf[:, k * F:(k + 1) * F]
+    def b_blk(k, h=None):
+        if h is None:
+            return T.bbuf[:, k * F:(k + 1) * F]
+        return T.bbuf[:, k * F + h * H:k * F + (h + 1) * H]
 
-    def b_sem(k):
-        return sem["b%d" % k]
+    def b_sem(k, h):
+        return sem["b%d_%d" % (k, h)]
 
-    via = {}
-    for k in range(GR):
-        for q in range(GR):
-            if q != k and not topo.may_write(col[k], col[q]):
-                via[(k, q)] = _relay(topo, col, k, q)
-    my_relays = [p for (k, q), p in via.items() if k == i]
-    direct = [q for q in range(GR) if q != i and topo.may_write(core, col[q])]
-    direct.sort(key=lambda q: 0 if q in my_relays else 1)
-    passing = [(k, q) for (k, q), p in via.items() if p == i]
-    first = [k for (k, q) in passing]
-    order = [i] + first + [k for k in range(GR) if k != i and k not in first and (k, i) not in via] \
-        + [k for k in range(GR) if (k, i) in via]
+    far = [q for q in range(GR) if q != i and not topo.may_write(core, col[q])][0]
+    cab = _relay(topo, col, i, far)
+    mate = [q for q in range(GR) if q not in (i, far, cab)][0]
+    full = topo.mask(core, col[cab]) & topo.mask(core, col[mate])
+    e_cab, e_sw = _split(full)
+    n_half, n_full = _engines(e_cab), _engines(full)
 
     g.sync.dma_start(T.astage[:], T.a[:]).then_inc(sem.a_st, 16)
-    g.scalar.dma_start(b_blk(i), T.b[:]).then_inc(b_sem(i), 16)
+    g.scalar.dma_start(b_blk(i, 0), T.b[:, 0:H]).then_inc(b_sem(i, 0), 16)
+    g.scalar.dma_start(b_blk(i, 1), T.b[:, H:F]).then_inc(b_sem(i, 1), 16)
     g.sync.dma_start(a_blk(j), T.a[:]).then_inc(sem.a_ld, 16)
 
     sent = 0
@@ -81,18 +83,20 @@ def rank_program(g, core, T, topo):
                        local_sem=sem.sent)
     sent += _engines(amask)
 
-    def send_b(k, q):
+    def send(ap, s, q, m):
         rid, pid = topo.addr(col[q], core)
-        m = topo.mask(core, col[q])
-        g.remote_dma(b_blk(k), b_blk(k), b_sem(k), sem.sent, pid, rid, m)
+        g.remote_dma(ap, ap, s, sem.sent, pid, rid, m)
         return _engines(m)
 
-    g.wait_ge(b_sem(i), 16)
-    for q in direct:
-        sent += send_b(i, q)
-    for (k, q) in passing:
-        g.wait_ge(b_sem(k), _engines(topo.mask(col[k], core)))
-        sent += send_b(k, q)
+    g.wait_ge(b_sem(i, 0), 16)
+    sent += send(b_blk(i, 0), b_sem(i, 0), cab, e_cab)
+    g.wait_ge(b_sem(i, 1), 16)
+    sent += send(b_blk(i, 1), b_sem(i, 1), cab, e_cab)
+    sent += send(b_blk(i), b_sem(i, 0), mate, e_sw)
+    g.wait_ge(b_sem(cab, 0), n_half)
+    sent += send(b_blk(cab, 0), b_sem(cab, 0), mate, e_sw)
+    g.wait_ge(b_sem(cab, 1), n_half)
+    sent += send(b_blk(cab, 1), b_sem(cab, 1), mate, full)
 
     a_in = sum(_engines(topo.mask(c, core)) for c in peers)
     g.sync.wait_ge(sem.a_arr, a_in)
@@ -104,20 +108,20 @@ def rank_program(g, core, T, topo):
             queues[n % 2].dma_start(a_blk(k), T.aland[k]).then_inc(sem.a_ld, 16)
             n += 1
 
+    acc = [T.acc0[:, 0:H], T.acc1[:, 0:H]]
+    steps = [(i, 0, 0, 16), (i, 1, 1, 16), (cab, 0, 0, n_half), (mate, 0, 0, n_half), (mate, 1, 0, n_half),
+             (cab, 1, 1, n_half), (far, 0, 0, n_half), (far, 1, 1, n_full)]
     g.tensor.wait_ge(sem.a_ld, 16 * GC)
-    for n, k in enumerate(order):
-        if k == i:
-            need = 16
-        elif (k, i) in via:
-            need = _engines(topo.mask(col[via[(k, i)]], core))
-        else:
-            need = _engines(topo.mask(col[k], core))
-        g.tensor.wait_ge(b_sem(k), need)
-        mm = g.tensor.matmul(T.acc[:], a_blk(k), b_blk(k), start=(n == 0), stop=(n == GR - 1))
-    mm.then_inc(sem.mm, 1)
-    g.vector.wait_ge(sem.mm, 1)
-    g.vector.tensor_copy(T.ysb[:], T.acc[:]).then_inc(sem.cp, 1)
-    g.sync.wait_ge(sem.cp, 1)
-    g.sync.dma_start(T.y[:], T.ysb[:]).then_inc(sem.st, 16)
-    g.sync.wait_ge(sem.st, 16)
+    for (k, h, sh, need) in steps:
+        g.tensor.wait_ge(b_sem(k, sh), need)
+        mm = g.tensor.matmul(acc[h], a_blk(k), b_blk(k, h), start=(k == i), stop=(k == far))
+        if k == far:
+            mm.then_inc(sem["mm%d" % h], 1)
+    out_q = [g.sync, g.scalar]
+    for h in range(2):
+        g.vector.wait_ge(sem["mm%d" % h], 1)
+        g.vector.tensor_copy(T.ysb[:, h * H:(h + 1) * H], acc[h]).then_inc(sem["cp%d" % h], 1)
+        out_q[h].wait_ge(sem["cp%d" % h], 1)
+        out_q[h].dma_start(T.y[:, h * H:(h + 1) * H], T.ysb[:, h * H:(h + 1) * H]).then_inc(sem["st%d" % h], 16)
+        out_q[h].wait_ge(sem["st%d" % h], 16)
     g.wait_ge(sem.sent, sent)

@@ -1,27 +1,34 @@
 from concourse.bass import DstId, RemoteDMATransfer
 
 GR, GC, F = 4, 4, 512
-H = F // 2
+BLK = [(0, 320), (320, 512)]
+GRP = [(0, 320, 0), (320, 416, 1), (416, 512, 1)]
+WORLD = 512
 
 SCRATCH = {
     "astage": ("dram", [128, 128], "bfloat16"),
-    "aland": ("dram", [GC, 128, 128], "bfloat16"),
+    "ahelp": ("dram", [128, 128], "bfloat16"),
     "abuf": ("sbuf", [128, GC * 128], "bfloat16"),
     "bbuf": ("sbuf", [128, GR * F], "bfloat16"),
     "ysb": ("sbuf", [128, F], "bfloat16"),
     "acc0": ("psum", [128, F], "float32"),
     "acc1": ("psum", [128, F], "float32"),
+    "acc2": ("psum", [128, F], "float32"),
 }
-SEMAPHORES = ["a_st", "a_arr", "a_ld", "sent", "mm0", "mm1", "cp0", "cp1", "st0", "st1"] \
-    + ["b%d_%d" % (k, h) for k in range(GR) for h in range(2)]
+SEMAPHORES = ["a_st", "h_arr", "sent", "mm0", "mm1", "mm2", "cp0", "cp1", "st0", "st1"] \
+    + ["a%d" % k for k in range(GC)] + ["b%d_%d" % (k, h) for k in range(GR) for h in range(2)]
 
 
 def _engines(mask):
     return bin(mask).count("1")
 
 
+def _bits(mask):
+    return [b for b in range(16) if (mask >> b) & 1]
+
+
 def _split(mask):
-    bits = [b for b in range(16) if (mask >> b) & 1]
+    bits = _bits(mask)
     return sum(1 << b for b in bits[0::2]), sum(1 << b for b in bits[1::2])
 
 
@@ -36,22 +43,61 @@ def _relay(topo, col, k, q):
     raise ValueError("no relay")
 
 
+def _row_peers(T, rc):
+    r = T.rank_of(rc)
+    return [T.cores[(r // GC) * GC + k] for k in range(GC) if k != r % GC]
+
+
+def _helpers(T, topo, rc):
+    peers = _row_peers(T, rc)
+    out = [c for c in range(WORLD)
+           if c != rc and topo.host(c) == topo.host(rc) and topo.chip(c) == topo.chip(rc)
+           and topo.die(c) != topo.die(rc) and T.rank_of(c) is None
+           and all(topo.may_write(c, p) for p in peers)]
+    return out[:len(peers)]
+
+
+def _a_mask(topo, rc, hs, off_chip_peer):
+    on = topo.mask(rc, hs[0])
+    for c in hs:
+        on &= topo.mask(rc, c)
+    return sum(1 << b for b in _bits(on & ~topo.mask(rc, off_chip_peer))[0::2][:4])
+
+
+def helper_program(g, core, T, topo):
+    owner = [rc for rc in T.cores if topo.host(rc) == topo.host(core) and topo.chip(rc) == topo.chip(core)]
+    if not owner:
+        return
+    rc = owner[0]
+    hs = _helpers(T, topo, rc)
+    if core not in hs:
+        return
+    peer = _row_peers(T, rc)[hs.index(core)]
+    k = T.rank_of(rc) % GC
+    m = topo.mask(core, peer)
+    rid, pid = topo.addr(peer, core)
+    g.wait_ge(T.sem.h_arr, _engines(_a_mask(topo, rc, hs, peer)))
+    g.remote_dma(T.abuf[:, k * 128:(k + 1) * 128], T.ahelp[:], T.sem["a%d" % k], T.sem.sent, pid, rid, m)
+    g.wait_ge(T.sem.sent, _engines(m))
+
+
 def rank_program(g, core, T, topo):
     rank = T.rank_of(core)
     if rank is None:
+        helper_program(g, core, T, topo)
         return
     i, j = rank // GC, rank % GC
-    row = [T.cores[i * GC + k] for k in range(GC)]
     col = [T.cores[k * GC + j] for k in range(GR)]
     sem = T.sem
 
     def a_blk(k):
         return T.abuf[:, k * 128:(k + 1) * 128]
 
-    def b_blk(k, h=None):
-        if h is None:
-            return T.bbuf[:, k * F:(k + 1) * F]
-        return T.bbuf[:, k * F + h * H:k * F + (h + 1) * H]
+    def b_cols(k, lo, hi):
+        return T.bbuf[:, k * F + lo:k * F + hi]
+
+    def b_blk(k, h):
+        return b_cols(k, BLK[h][0], BLK[h][1])
 
     def b_sem(k, h):
         return sem["b%d_%d" % (k, h)]
@@ -64,24 +110,11 @@ def rank_program(g, core, T, topo):
     n_half, n_full = _engines(e_cab), _engines(full)
 
     g.sync.dma_start(T.astage[:], T.a[:]).then_inc(sem.a_st, 16)
-    g.scalar.dma_start(b_blk(i, 0), T.b[:, 0:H]).then_inc(b_sem(i, 0), 16)
-    g.scalar.dma_start(b_blk(i, 1), T.b[:, H:F]).then_inc(b_sem(i, 1), 16)
-    g.sync.dma_start(a_blk(j), T.a[:]).then_inc(sem.a_ld, 16)
+    for h in range(2):
+        g.scalar.dma_start(b_blk(i, h), T.b[:, BLK[h][0]:BLK[h][1]]).then_inc(b_sem(i, h), 16)
+    g.sync.dma_start(a_blk(j), T.a[:]).then_inc(sem["a%d" % j], 16)
 
     sent = 0
-    peers = [c for c in row if c != core]
-    amask = topo.mask(core, peers[0])
-    for c in peers:
-        amask &= topo.mask(core, c)
-    ids = []
-    for c in peers:
-        rid, pid = topo.addr(c, core)
-        ids.append(DstId(rid=rid, pnc=pid))
-    g.wait_ge(sem.a_st, 16)
-    g.remote_dma_fused([RemoteDMATransfer(dst_ids=ids, dma_engine_mask=amask, remote_sem=sem.a_arr,
-                                          srcs=[T.astage[:]], dsts=[T.aland[j] for _ in peers], alu_op=0)],
-                       local_sem=sem.sent)
-    sent += _engines(amask)
 
     def send(ap, s, q, m):
         rid, pid = topo.addr(col[q], core)
@@ -90,38 +123,53 @@ def rank_program(g, core, T, topo):
 
     g.wait_ge(b_sem(i, 0), 16)
     sent += send(b_blk(i, 0), b_sem(i, 0), cab, e_cab)
+
+    hs = _helpers(T, topo, core)
+    amask = _a_mask(topo, core, hs, _row_peers(T, core)[0])
+    ids = []
+    for c in hs:
+        rid, pid = topo.addr(c, core)
+        ids.append(DstId(rid=rid, pnc=pid))
+    g.wait_ge(sem.a_st, 16)
+    g.remote_dma_fused([RemoteDMATransfer(dst_ids=ids, dma_engine_mask=amask, remote_sem=sem.h_arr,
+                                          srcs=[T.astage[:]], dsts=[T.ahelp[:] for _ in hs], alu_op=0)],
+                       local_sem=sem.sent)
+    sent += _engines(amask)
+
     g.wait_ge(b_sem(i, 1), 16)
     sent += send(b_blk(i, 1), b_sem(i, 1), cab, e_cab)
-    sent += send(b_blk(i), b_sem(i, 0), mate, e_sw)
+    sent += send(b_cols(i, 0, F), b_sem(i, 0), mate, e_sw)
     g.wait_ge(b_sem(cab, 0), n_half)
     sent += send(b_blk(cab, 0), b_sem(cab, 0), mate, e_sw)
     g.wait_ge(b_sem(cab, 1), n_half)
     sent += send(b_blk(cab, 1), b_sem(cab, 1), mate, full)
 
-    a_in = sum(_engines(topo.mask(c, core)) for c in peers)
-    g.sync.wait_ge(sem.a_arr, a_in)
-    g.scalar.wait_ge(sem.a_arr, a_in)
-    queues = [g.scalar, g.sync]
-    n = 0
-    for k in range(GC):
-        if k != j:
-            queues[n % 2].dma_start(a_blk(k), T.aland[k]).then_inc(sem.a_ld, 16)
-            n += 1
-
-    acc = [T.acc0[:, 0:H], T.acc1[:, 0:H]]
+    acc = [T["acc%d" % n][:, 0:hi - lo] for n, (lo, hi, h) in enumerate(GRP)]
     steps = [(i, 0, 0, 16), (i, 1, 1, 16), (cab, 0, 0, n_half), (mate, 0, 0, n_half), (mate, 1, 0, n_half),
              (cab, 1, 1, n_half), (far, 0, 0, n_half), (far, 1, 1, n_full)]
-    g.tensor.wait_ge(sem.a_ld, 16 * GC)
+    if j != far:
+        steps = [s for s in steps if s[0] == j] + [s for s in steps if s[0] != j]
+    begun = [False for _ in GRP]
     for (k, h, sh, need) in steps:
+        if k == j:
+            g.tensor.wait_ge(sem["a%d" % k], 16)
+        else:
+            src = T.cores[i * GC + k]
+            g.tensor.wait_ge(sem["a%d" % k], _engines(topo.mask(_helpers(T, topo, src)[0], core)))
         g.tensor.wait_ge(b_sem(k, sh), need)
-        mm = g.tensor.matmul(acc[h], a_blk(k), b_blk(k, h), start=(k == i), stop=(k == far))
-        if k == far:
-            mm.then_inc(sem["mm%d" % h], 1)
+        for n, (lo, hi, gh) in enumerate(GRP):
+            if gh != h:
+                continue
+            mm = g.tensor.matmul(acc[n], a_blk(k), b_cols(k, lo, hi), start=(not begun[n]), stop=(k == far))
+            begun[n] = True
+            if k == far:
+                mm.then_inc(sem["mm%d" % n], 1)
+    for n, (lo, hi, h) in enumerate(GRP):
+        g.vector.wait_ge(sem["mm%d" % n], 1)
+        g.vector.tensor_copy(T.ysb[:, lo:hi], acc[n]).then_inc(sem["cp%d" % h], 1)
     out_q = [g.sync, g.scalar]
-    for h in range(2):
-        g.vector.wait_ge(sem["mm%d" % h], 1)
-        g.vector.tensor_copy(T.ysb[:, h * H:(h + 1) * H], acc[h]).then_inc(sem["cp%d" % h], 1)
-        out_q[h].wait_ge(sem["cp%d" % h], 1)
-        out_q[h].dma_start(T.y[:, h * H:(h + 1) * H], T.ysb[:, h * H:(h + 1) * H]).then_inc(sem["st%d" % h], 16)
+    for h, (lo, hi) in enumerate(BLK):
+        out_q[h].wait_ge(sem["cp%d" % h], sum(1 for x in GRP if x[2] == h))
+        out_q[h].dma_start(T.y[:, lo:hi], T.ysb[:, lo:hi]).then_inc(sem["st%d" % h], 16)
         out_q[h].wait_ge(sem["st%d" % h], 16)
     g.wait_ge(sem.sent, sent)

from concourse.bass import DstId, RemoteDMATransfer

GR, GC, F = 4, 4, 512
BLK = [(0, 320), (320, 512)]
GRP = [(0, 320, 0), (320, 416, 1), (416, 512, 1)]
WORLD = 512

SCRATCH = {
    "astage": ("dram", [128, 128], "bfloat16"),
    "ahelp": ("dram", [128, 128], "bfloat16"),
    "abuf": ("sbuf", [128, GC * 128], "bfloat16"),
    "bbuf": ("sbuf", [128, GR * F], "bfloat16"),
    "ysb": ("sbuf", [128, F], "bfloat16"),
    "acc0": ("psum", [128, F], "float32"),
    "acc1": ("psum", [128, F], "float32"),
    "acc2": ("psum", [128, F], "float32"),
}
SEMAPHORES = ["a_st", "h_arr", "sent", "mm0", "mm1", "mm2", "cp0", "cp1", "st0", "st1"] \
    + ["a%d" % k for k in range(GC)] + ["b%d_%d" % (k, h) for k in range(GR) for h in range(2)]


def _engines(mask):
    return bin(mask).count("1")


def _bits(mask):
    return [b for b in range(16) if (mask >> b) & 1]


def _split(mask):
    bits = _bits(mask)
    return sum(1 << b for b in bits[0::2]), sum(1 << b for b in bits[1::2])


def _relay(topo, col, k, q):
    for p in range(len(col)):
        if p in (k, q):
            continue
        if not (topo.may_write(col[k], col[p]) and topo.may_write(col[p], col[q])):
            continue
        if topo.rack(topo.host(col[k])) != topo.rack(topo.host(col[p])):
            return p
    raise ValueError("no relay")


def _row_peers(T, rc):
    r = T.rank_of(rc)
    return [T.cores[(r // GC) * GC + k] for k in range(GC) if k != r % GC]


def _helpers(T, topo, rc):
    peers = _row_peers(T, rc)
    out = [c for c in range(WORLD)
           if c != rc and topo.host(c) == topo.host(rc) and topo.chip(c) == topo.chip(rc)
           and topo.die(c) != topo.die(rc) and T.rank_of(c) is None
           and all(topo.may_write(c, p) for p in peers)]
    return out[:len(peers)]


def _a_mask(topo, rc, hs, off_chip_peer):
    on = topo.mask(rc, hs[0])
    for c in hs:
        on &= topo.mask(rc, c)
    return sum(1 << b for b in _bits(on & ~topo.mask(rc, off_chip_peer))[0::2][:4])


def helper_program(g, core, T, topo):
    owner = [rc for rc in T.cores if topo.host(rc) == topo.host(core) and topo.chip(rc) == topo.chip(core)]
    if not owner:
        return
    rc = owner[0]
    hs = _helpers(T, topo, rc)
    if core not in hs:
        return
    peer = _row_peers(T, rc)[hs.index(core)]
    k = T.rank_of(rc) % GC
    m = topo.mask(core, peer)
    rid, pid = topo.addr(peer, core)
    g.wait_ge(T.sem.h_arr, _engines(_a_mask(topo, rc, hs, peer)))
    g.remote_dma(T.abuf[:, k * 128:(k + 1) * 128], T.ahelp[:], T.sem["a%d" % k], T.sem.sent, pid, rid, m)
    g.wait_ge(T.sem.sent, _engines(m))


def rank_program(g, core, T, topo):
    rank = T.rank_of(core)
    if rank is None:
        helper_program(g, core, T, topo)
        return
    i, j = rank // GC, rank % GC
    col = [T.cores[k * GC + j] for k in range(GR)]
    sem = T.sem

    def a_blk(k):
        return T.abuf[:, k * 128:(k + 1) * 128]

    def b_cols(k, lo, hi):
        return T.bbuf[:, k * F + lo:k * F + hi]

    def b_blk(k, h):
        return b_cols(k, BLK[h][0], BLK[h][1])

    def b_sem(k, h):
        return sem["b%d_%d" % (k, h)]

    far = [q for q in range(GR) if q != i and not topo.may_write(core, col[q])][0]
    cab = _relay(topo, col, i, far)
    mate = [q for q in range(GR) if q not in (i, far, cab)][0]
    full = topo.mask(core, col[cab]) & topo.mask(core, col[mate])
    e_cab, e_sw = _split(full)
    n_half, n_full = _engines(e_cab), _engines(full)

    g.sync.dma_start(T.astage[:], T.a[:]).then_inc(sem.a_st, 16)
    for h in range(2):
        g.scalar.dma_start(b_blk(i, h), T.b[:, BLK[h][0]:BLK[h][1]]).then_inc(b_sem(i, h), 16)
    g.sync.dma_start(a_blk(j), T.a[:]).then_inc(sem["a%d" % j], 16)

    sent = 0

    def send(ap, s, q, m):
        rid, pid = topo.addr(col[q], core)
        g.remote_dma(ap, ap, s, sem.sent, pid, rid, m)
        return _engines(m)

    g.wait_ge(b_sem(i, 0), 16)
    sent += send(b_blk(i, 0), b_sem(i, 0), cab, e_cab)

    hs = _helpers(T, topo, core)
    amask = _a_mask(topo, core, hs, _row_peers(T, core)[0])
    ids = []
    for c in hs:
        rid, pid = topo.addr(c, core)
        ids.append(DstId(rid=rid, pnc=pid))
    g.wait_ge(sem.a_st, 16)
    g.remote_dma_fused([RemoteDMATransfer(dst_ids=ids, dma_engine_mask=amask, remote_sem=sem.h_arr,
                                          srcs=[T.astage[:]], dsts=[T.ahelp[:] for _ in hs], alu_op=0)],
                       local_sem=sem.sent)
    sent += _engines(amask)

    g.wait_ge(b_sem(i, 1), 16)
    sent += send(b_blk(i, 1), b_sem(i, 1), cab, e_cab)
    sent += send(b_cols(i, 0, F), b_sem(i, 0), mate, e_sw)
    g.wait_ge(b_sem(cab, 0), n_half)
    sent += send(b_blk(cab, 0), b_sem(cab, 0), mate, e_sw)
    g.wait_ge(b_sem(cab, 1), n_half)
    sent += send(b_blk(cab, 1), b_sem(cab, 1), mate, full)

    acc = [T["acc%d" % n][:, 0:hi - lo] for n, (lo, hi, h) in enumerate(GRP)]
    steps = [(i, 0, 0, 16), (i, 1, 1, 16), (cab, 0, 0, n_half), (mate, 0, 0, n_half), (mate, 1, 0, n_half),
             (cab, 1, 1, n_half), (far, 0, 0, n_half), (far, 1, 1, n_full)]
    if j != far:
        steps = [s for s in steps if s[0] == j] + [s for s in steps if s[0] != j]
    begun = [False for _ in GRP]
    for (k, h, sh, need) in steps:
        if k == j:
            g.tensor.wait_ge(sem["a%d" % k], 16)
        else:
            src = T.cores[i * GC + k]
            g.tensor.wait_ge(sem["a%d" % k], _engines(topo.mask(_helpers(T, topo, src)[0], core)))
        g.tensor.wait_ge(b_sem(k, sh), need)
        for n, (lo, hi, gh) in enumerate(GRP):
            if gh != h:
                continue
            mm = g.tensor.matmul(acc[n], a_blk(k), b_cols(k, lo, hi), start=(not begun[n]), stop=(k == far))
            begun[n] = True
            if k == far:
                mm.then_inc(sem["mm%d" % n], 1)
    for n, (lo, hi, h) in enumerate(GRP):
        g.vector.wait_ge(sem["mm%d" % n], 1)
        g.vector.tensor_copy(T.ysb[:, lo:hi], acc[n]).then_inc(sem["cp%d" % h], 1)
    out_q = [g.sync, g.scalar]
    for h, (lo, hi) in enumerate(BLK):
        out_q[h].wait_ge(sem["cp%d" % h], sum(1 for x in GRP if x[2] == h))
        out_q[h].dma_start(T.y[:, lo:hi], T.ysb[:, lo:hi]).then_inc(sem["st%d" % h], 16)
        out_q[h].wait_ge(sem["st%d" % h], 16)
    g.wait_ge(sem.sent, sent)
